import numpy as np, ml_dtypes
CORES = [9,25,41,57]
N = 4
import mx_ref
BF = ml_dtypes.bfloat16
def gentries(a):
    return np.ascontiguousarray(a.reshape(8, 16, -1).transpose(0, 2, 1)).reshape(8, -1)
def gtable(e):
    e = np.asarray(e); return np.ascontiguousarray(e.reshape(8, -1, 16).transpose(0, 2, 1)).reshape(128, -1).astype(np.int32)
def gcols(t, e):
    v = np.concatenate([t.reshape(8, 16, -1, 4), np.zeros((8, 16, 1, 4), BF)], axis=2)
    return np.ascontiguousarray(np.stack([v[g][:, e[g]] for g in range(8)])).reshape(128, -1)
def gpick(z, e):
    return np.concatenate([z[16 * g:16 * g + 16][:, e[g]] for g in range(8)])
def tile(rs):
    return np.stack(rs, axis=2).reshape(128, -1).astype(BF)
def pick(q, e):
    c = np.concatenate([q[0].reshape(128, -1, 4), np.zeros((128, 1, 4), np.uint8)], axis=1); s = np.concatenate([q[1], np.ones((16, 1), np.uint8)], axis=1)
    return (np.ascontiguousarray(c[:, e].reshape(128, -1)), np.ascontiguousarray(s[:, e]))
def join(*qs):
    return (np.concatenate([q[0] for q in qs], axis=1), np.concatenate([q[1] for q in qs], axis=1))
def put(q, e, v):
    c, s = q[0].reshape(128, -1, 4).copy(), q[1].copy(); c[:, e] = v[0].reshape(128, -1, 4); s[:, e] = v[1]
    return (c.reshape(128, -1), s)
def pk(c, s):
    return (np.ascontiguousarray(c), mx_ref.live(s))
def emit(q):
    return q[0], q[1]
def packed(v, rng):
    q = [mx_ref.quantize(np.ascontiguousarray(v[r])) for r in range(N)]
    return np.stack([a for a, b in q]), np.stack([mx_ref.plane(b, rng) for a, b in q])
def values_of_codes():
    e, c = np.zeros((128, 128, 4), np.float32), np.zeros((128, 2, 4), np.uint8)
    e[np.arange(128), np.arange(128), 0] = 1
    c[:127, :, 0] = np.arange(256).reshape(2, 128).T[:127]
    return mx_ref.matmul(mx_ref.quantize(e.reshape(128, 512).astype(BF)), (c.reshape(128, 8), np.full((16, 2), 127, np.uint8))).T.reshape(-1).astype(np.float64)
CODE_VALUE, SCALE_VALUE = values_of_codes(), 2.0 ** (np.arange(256) - 127.0)
def decode(q):
    return (CODE_VALUE[q[0]].reshape(16, 8, -1, 4) * SCALE_VALUE[q[1]][:, None, :, None] + 0.0).reshape(128, -1).astype(np.float32)
def f(rng, *shape):
    return mx_ref.flush((rng.standard_normal(shape, dtype=np.float32) * np.exp2(rng.integers(-2, 3, shape[:-1] + (1,)))).astype(BF))
def wide(rng, *shape, cols=0):
    v = rng.standard_normal(shape, dtype=np.float32) * np.exp2(rng.integers(-12, 13, shape)).astype(np.float32)
    if cols: v *= np.repeat(np.exp2(rng.integers(-cols, cols + 1, shape[:-2] + (1, shape[-1] // 4))) * (rng.random(shape[:-2] + (1, shape[-1] // 4)) > 0.0625), 4, axis=-1).astype(np.float32)
    return mx_ref.flush(v.astype(BF))
C = 384
STEP = [1, 2, 3]
def numbers_of(rng):
    return {"x": np.array(f(rng, N, 128, 4 * C)), "u": np.array(f(rng, N, 128, 512)), "v": np.array(f(rng, N, 128, 512))}
def orders(rng):
    return rng.permuted(np.tile(np.arange(C), (N, 8, 1)), axis=2)
def mates(rng):
    e = orders(rng)
    m = np.zeros_like(e)
    np.put_along_axis(m, e[:, :, 0::2], e[:, :, 1::2], axis=2)
    np.put_along_axis(m, e[:, :, 1::2], e[:, :, 0::2], axis=2)
    return m
def stored(c, a, m):
    return {"cl": np.stack([gtable(c[r]) for r in range(N)]), "pl": np.stack([gtable(a[r]) for r in range(N)]), "ml": np.stack([gtable(m[r]) for r in range(N)])}
def lists(rng):
    return stored(orders(rng), orders(rng), mates(rng))
def layers(rng, still=[]):
    w = np.array(f(rng, N, 128, 2048)).reshape(N, 8, 16, 4, 8, 16, 4)
    for i in still:
        w[:, :, i] = 0
        w[:, :, :, :, :, i] = 0
    return w
def weights(rng, w):
    c, s = packed(np.ascontiguousarray(w).reshape(N, 128, 2048), rng)
    return {"wc": c, "ws": s}
def setup_inputs(rng):
    return {**numbers_of(rng), **lists(rng), **weights(rng, layers(rng))}
def setup_inputs_ties(rng):
    d = numbers_of(rng)
    o = rng.permutation(N)
    k = rng.integers(0, 4, (N, 8, C))
    k[o[1]] -= 4
    k[o[2], rng.permutation(8)[:4]] = 1
    x = d["x"].reshape(N, 8, 16, C, 4)
    x[:, :, 0] = 0
    x[:, :, 0, :, 0] = k.astype(np.float32).astype(BF)
    u = d["u"].reshape(N, 128, 128, 4)
    u[:, :, ::16] = 0
    for r in range(N):
        for h in range(0, 128, 16): u[r, h, h, 0] = 0.0 if r == o[0] else 1.0
    c, a, m = orders(rng), orders(rng), mates(rng)
    c[o[3]] = m[o[3]]
    return {"x": x.reshape(N, 128, 4 * C), "u": u.reshape(N, 128, 512), "v": d["v"], **stored(c, a, m), **weights(rng, layers(rng, [0]))}
def setup_inputs_near(rng):
    d = numbers_of(rng)
    x = d["x"].astype(np.float32).reshape(N, 8, 16, C, 4)
    x[:, :, 0] = 0
    x[:, :, 8:] = 0
    u = d["u"].reshape(N, 128, 128, 4)
    u[:, :, ::16] = 0
    o = (np.arange(N) + rng.integers(4)) % 4
    for r in range(N):
        c = rng.choice([-1.0, 1.0], (8, 1))
        s = rng.integers(0, 16, (8, C))
        digits = ((s[:, :, None] >> np.arange(4)) & 1) * np.exp2(np.arange(4) - 23.0)
        if o[r] < 2:
            x[r, :, 0, :, 0] = c
            x[r, :, 8] = digits
            x[r, :, 11, :, 0] = 2.0 ** -10
        elif o[r] == 2: x[r, :, 8] = digits * rng.choice([-1.0, 1.0], (8, C, 1))
        else:
            x[r, :, 8, :, 0] = np.where(s < 8, 1.25, 0.0) * 2.0 ** -29 * c
            x[r, :, 9, :, 0] = np.where(s < 8, 0.0, 1.125) * 2.0 ** -29 * c
            for g in rng.permutation(8)[:4]:
                e = rng.choice([-1.0, 1.0], C) * 2.0 ** -29
                x[r, g, 8, :, 0] = 1.25 * e
                x[r, g, 9, :, 0] = -1.125 * e
        if o[r] >= 2: x[r, :, 12, :, 0] = np.where(rng.random((8, C)) < 0.5, 1.0, 1.5) * 2.0 ** -30
        at = [0, C - 1, int(rng.integers(C)), int(rng.integers(C))]
        for g, j in zip(rng.permutation(8)[:4], at): x[r, g, 0, j, 0] = 2.0 ** 29 * rng.choice([-1.0, 1.0])
        k = 1.0 if o[r] == 0 else 2.0 ** -30
        for h in range(0, 128, 16):
            u[r, h, h, 0] = k if o[r] < 2 else 1.0
            if o[r] < 2: u[r, h + 11, h, 0] = k
            if o[r] < 3: u[r, h + 8, h] = k
            else:
                u[r, h + 8, h, 0] = k
                u[r, h + 9, h, 0] = 1.125 * k
                u[r, h + 10, h, 0] = k
    w = layers(rng, [0, 8, 9, 10, 11, 12, 13, 14, 15])
    for g in range(8): w[:, g, 12, 0, g, 10, 0] = 2.0 ** -8
    return {"x": x.reshape(N, 128, 4 * C).astype(BF), "u": u.reshape(N, 128, 512), "v": d["v"], **lists(rng), **weights(rng, w)}
def setup_inputs_odd(rng):
    d = numbers_of(rng)
    k = (N, 8, 2, 8, C, 4)
    x = (1.0 + (2 * rng.integers(0, 64, k) + 1) * 2.0 ** -7) * np.exp2(-rng.integers(0, 7, k).astype(np.float64)) * rng.choice([-1.0, 1.0], k)
    x[:, :, 0, 0, :, 0] = 1.96875 * 2.0 ** 8 * rng.choice([-1.0, 1.0], (N, 8, C))
    x[:, :, 1, 0, :, 0] = np.where(rng.random((N, 8, C)) < 0.5, 1.875, 0.09375) * 2.0 ** 8
    u = d["u"].reshape(N, 8, 2, 8, 128, 4)
    u[:, :, :, 0, ::16] = 0
    for r in range(N):
        for i, g in enumerate(rng.permutation(8)[:4]):
            x[r, g, 0, 1, :, 0] = (8 + rng.integers(0, 2, C)) * 2.0 ** (i - 8)
            u[r, :, :, :, 16 * g] = 0
            u[r, g, 0, 1, 16 * g, 0] = 1.0
    return {"x": x.astype(np.float32).reshape(N, 128, 4 * C).astype(BF), "u": u.reshape(N, 128, 512), "v": d["v"], **lists(rng), **weights(rng, layers(rng, [0, 8]))}
def setup_inputs_ends(rng):
    d = numbers_of(rng)
    x = np.zeros((N, 8, 16, C, 4))
    u = d["u"].astype(np.float32).reshape(N, 128, 128, 4)
    v = d["v"].astype(np.float32)
    w = np.zeros((N, 128, 4, 128, 4), np.float32)
    o, e = rng.permutation(N) % 4, rng.permutation(N) % 4
    i = np.arange(128)
    for r in range(N):
        h = rng.permutation(8)
        s = np.where(h < 2, 0.0, h % 2 * 2.0 - 1.0)[None, :, None]
        high = (0.9 + 0.1 * rng.random((8, 16, C, 4))) * 2.0 ** 30
        if o[r] == 0: x[r] = -high
        if o[r] == 1: x[r] = high * rng.choice([-1.0, 1.0], (1, 1, C, 1))
        if o[r] == 2: x[r] = -(1.0 + 0.125 * rng.integers(0, 8, (8, 16, C, 4))) * 2.0 ** -30
        if o[r] == 3: x[r] = d["x"][r].astype(np.float32).reshape(8, 16, C, 4)[:, :, :1]
        if o[r] < 2:
            x[r, :, 15] = 0
            u[r, :, ::16] = s * (0.9 + 0.1 * rng.random((128, 8, 4))) * 2.0 ** 30
            v[r] = rng.choice([-1.0, 1.0], (128, 512)) * (0.9 + 0.1 * rng.random((128, 512))) * 2.0 ** 30
        if o[r] == 2:
            u[r, :, ::16] = s * (1.0 + 0.125 * rng.integers(0, 8, (128, 8, 4))) * 2.0 ** -30
            v[r] = rng.choice([-1.0, 1.0], (128, 512)) * (1.0 + 0.125 * rng.integers(0, 8, (128, 512))) * 2.0 ** -30
        if o[r] == 3: u[r, :, ::16] *= np.abs(s).astype(np.float32)
        k = np.full(128, [-0.125, -0.125, 0.25, 2.0 ** -8][o[r]])
        if o[r] >= 2: k[15::16] = 2.0 ** 8
        for b in range(4): w[r, i, b, i, b] = k
    c, a, m = orders(rng), orders(rng), mates(rng)
    j = np.arange(C)
    c[e == 0], m[e == 0] = j, j ^ 1
    c[e == 1], m[e == 1] = C - 1 - j, C - 1 - j
    c[e == 2], a[e == 2], m[e == 2] = C - 1 - j, j, (j + C // 2) % C
    return {"x": x.astype(np.float32).reshape(N, 128, 4 * C).astype(BF), "u": u.reshape(N, 128, 512).astype(BF), "v": v.astype(BF), **stored(c, a, m), **weights(rng, w.astype(BF))}
def setup_inputs_spread(rng):
    d = setup_inputs(rng)
    d["x"] = wide(rng, N, 128, 4 * C, cols=6)
    return d
def check_inputs(d):
    b = []
    for k in ("x", "u", "v"):
        a = np.abs(d[k].astype(np.float32))
        if not (np.isfinite(a).all() and ((a == 0) | (a >= 2.0 ** -30) & (a <= 2.0 ** 30)).all()): b.append("a value of " + k)
    j = np.arange(C)
    for k in ("cl", "pl", "ml"):
        for r in range(N):
            e = gentries(d[k][r])
            if not (np.sort(e, axis=1) == j).all(): b.append("a list of " + k)
            elif k == "ml" and ((at(e, e) != j) | (e == j)).any(): b.append("ml: mates")
    none, least, most = [emit(mx_ref.quantize(np.full((128, 16), k, np.float32).astype(BF)))[1][0, 0] for k in (0.0, 2.0 ** -8, 2.0 ** 8)]
    for r in range(N):
        if ((d["wc"][r] == 0x7F) | (d["wc"][r] == 0xFF)).any(): b.append("wc: a code that is no number")
        s = mx_ref.live(d["ws"][r])
        if ((s != none) & ((s < least) | (s > most))).any(): b.append("ws: a scale out of range")
        if (((d["wc"][r].reshape(16, 8, 512, 4) & 0x7F) != 0) & (s == none)[:, None, :, None]).any(): b.append("wc: a code other than zero under the scale of zeros")
    return b
def at(a, e):
    return np.take_along_axis(a, e, axis=1)
def above(s, a, b):
    return (at(s, a) > at(s, b)) | (at(s, a) == at(s, b)) & (a < b)
def reference(x, u, v, cl, pl, ml, wc, ws):
    qu = [mx_ref.quantize(u[r]) for r in range(N)]
    lay = [pk(wc[r], ws[r]) for r in range(N)]
    child, parent, mate = [gentries(cl[r]) for r in range(N)], [gentries(pl[r]) for r in range(N)], [gentries(ml[r]) for r in range(N)]
    j = np.tile(np.arange(C), (8, 1))
    now = [x[r] for r in range(N)]
    for step in STEP:
        t, z = [], []
        for r in range(N):
            q = mx_ref.quantize(now[r])
            s = mx_ref.matmul(qu[r], q)[::16] + np.float32(0.0)
            c, m = child[r], mate[r]
            o = np.where(above(s, j, m) == above(s, c, at(c, m)), c, at(c, m))
            new = np.argsort(o, axis=1)
            k = at(o, at(np.argsort(parent[r], axis=1), at(m, at(parent[r], new))))
            t.append(decode(q))
            p = t[r].astype(BF)
            z.append(mx_ref.quantize(((gcols(p, new).astype(np.float32) + gcols(p, k).astype(np.float32)) * np.float32(0.5)).astype(BF)))
            parent[r], mate[r] = new, k
        for r in range(N):
            h = [mx_ref.matmul(pick(lay[r], np.arange(128 * b, 128 * b + 128)), z[(r - step) % N]) * np.float32(0.03125) for b in range(4)]
            now[r] = tile([t[r][:, b::4] + gpick(h[b], parent[r]) for b in range(4)])
    y, co = np.zeros((N, 128, C), np.float32), np.zeros((N, 8, C), np.float32)
    oc, osc = np.zeros((N, 128, 4 * C), np.uint8), np.zeros((N, 16, C), np.uint8)
    for r in range(N):
        q = mx_ref.quantize(now[r])
        y[r] = mx_ref.matmul(mx_ref.quantize(v[r]), q)
        co[r] = mate[r]
        oc[r], osc[r] = emit(q)
    return {"y": y, "co": co, "oc": oc, "osc": osc}

@@ -1,0 +1,342 @@
+from concourse.mybir import dt, AluOpType, ActivationFunctionType
+
+C = 384
+L = 24
+HALF = C // 2
+ROUNDS = 3
+BIG = 2.0 ** 40
+
+SCRATCH = {
+    "uin": ("sbuf", [128, 512], "bfloat16"), "vin": ("sbuf", [128, 512], "bfloat16"),
+    "wcb": ("sbuf", [128, 512], "float8_e4m3fn_x4"), "wsb": ("sbuf", [128, 512], "uint8"),
+    "ones": ("sbuf", [128, 128], "bfloat16"), "diag": ("sbuf", [128, 128], "bfloat16"),
+    "eb": ("sbuf", [128, 2048], "bfloat16"), "qe": ("sbuf", [128, 512], "float8_e4m3fn_x4"), "se": ("sbuf", [128, 512], "uint8"),
+    "r16": ("sbuf", [128, 16], "int32"), "r15": ("sbuf", [128, 16], "int32"),
+    "mda": ("sbuf", [128, 16], "bfloat16"), "mdb": ("sbuf", [128, 16], "bfloat16"), "md": ("sbuf", [128, 2 * C], "bfloat16"),
+    "pcol": ("sbuf", [128, 1], "int32"), "p15": ("sbuf", [128, 1], "int32"), "p15f": ("sbuf", [128, 1], "float32"),
+    "fac": ("sbuf", [128, 1], "float32"), "thr": ("sbuf", [128, 1], "float32"),
+    "q24": ("sbuf", [128, L], "float32"), "uli": ("sbuf", [128, 8], "int32"), "ul": ("sbuf", [128, 8], "uint16"),
+    "scab": ("sbuf", [128, 2 * C], "bfloat16"), "ab": ("sbuf", [128, 2 * C], "bfloat16"),
+    "lou": ("sbuf", [128, 2 * L], "uint16"), "hiu": ("sbuf", [128, 2 * L], "uint16"),
+    "sw": ("sbuf", [128, C], "float32"), "gg": ("sbuf", [128, 2 * C], "float32"),
+    "tb": ("sbuf", [128, 4 * C], "bfloat16"), "tp": ("sbuf", [128, 4 * C], "bfloat16"),
+    "gb": ("sbuf", [128, 4 * C], "bfloat16"), "zt": ("sbuf", [128, 4 * C], "bfloat16"),
+    "qz": ("sbuf", [128, C], "float8_e4m3fn_x4"), "sz": ("sbuf", [128, C], "uint8"),
+    "rs": ("sbuf", [128, 4 * C], "float32"), "cof": ("sbuf", [128, C], "float32"), "yb": ("sbuf", [128, C], "float32"),
+}
+for _k in ("qu0", "qu", "qv"):
+    SCRATCH[_k] = ("sbuf", [128, 128], "float8_e4m3fn_x4")
+for _k in ("su0", "su", "sv"):
+    SCRATCH[_k] = ("sbuf", [128, 128], "uint8")
+for _k in ("cin", "minp", "pin"):
+    SCRATCH[_k] = ("sbuf", [128, L], "int32")
+for _k in ("cu", "mu", "au", "ciu", "acu", "fu", "alu", "beu", "wu"):
+    SCRATCH[_k] = ("sbuf", [128, L], "uint16")
+for _k in ("iob", "cb", "mb", "cmb", "cib", "aib", "acb", "bb", "bmb", "fb", "hb", "n0b", "shb", "alb", "gab", "wb", "kb", "sc0", "sc1", "sc2"):
+    SCRATCH[_k] = ("sbuf", [128, C], "bfloat16")
+for _k in ("base", "alt", "mn", "mx", "lt", "dd", "bits", "abv", "unl", "pr", "rr"):
+    SCRATCH[_k] = ("sbuf", [128, 2 * L], "float32")
+for _d in range(ROUNDS + 1):
+    SCRATCH["xt%d" % _d] = ("sbuf", [128, 4 * C], "bfloat16")
+    SCRATCH["qx%d" % _d] = ("sbuf", [128, C], "float8_e4m3fn_x4")
+    SCRATCH["sx%d" % _d] = ("sbuf", [128, C], "uint8")
+for _d in range(ROUNDS):
+    SCRATCH["lc%d" % _d] = ("sbuf", [128, C], "float8_e4m3fn_x4")
+    SCRATCH["ls%d" % _d] = ("sbuf", [128, C], "uint8")
+    SCRATCH["la%d" % _d] = ("sbuf", [128, L], "uint16")
+    SCRATCH["lk%d" % _d] = ("sbuf", [128, L], "uint16")
+    SCRATCH["off%d" % _d] = ("sbuf", [128, 2 * L], "uint16")
+    SCRATCH["ku%d" % _d] = ("sbuf", [128, L], "uint16")
+for _b in range(8):
+    SCRATCH["ps%d" % _b] = ("psum", [128, 512], "float32")
+
+SEMAPHORES = ["ev", "es", "et", "ep", "sent"] + ["d%d" % _k for _k in range(18)]
+SEMAPHORES += ["%s%d" % (_k, _d) for _d in range(ROUNDS) for _k in ("ac", "aa", "ak")]
+
+ADD, SUB, MUL, MIN, MAX = AluOpType.add, AluOpType.subtract, AluOpType.mult, AluOpType.min, AluOpType.max
+GE, GT, LT, EQ, NE = AluOpType.is_ge, AluOpType.is_gt, AluOpType.is_lt, AluOpType.is_equal, AluOpType.not_equal
+AND = AluOpType.bitwise_and
+COPY = ActivationFunctionType.Copy
+
+
+def rank_program(g, core, T, topo):
+    rank = T.rank_of(core)
+    if rank is None:
+        return
+    n = len(T.cores)
+    queue = {"v": g.vector, "s": g.scalar, "t": g.tensor, "p": g, "y": g.sync}
+    total, seen, wrote, read = {}, {}, {}, {}
+    ndma = [0]
+
+    def wait(q, toks):
+        need = {}
+        for s, k in toks:
+            need[s] = max(need.get(s, 0), k)
+        for s in need:
+            if seen.get((q, s), 0) < need[s]:
+                queue[q].wait_ge(T.sem[s], need[s])
+                seen[(q, s)] = need[s]
+
+    def before(q, rd, wr):
+        own = "e" + q
+        toks = [wrote[r] for r in rd if r in wrote]
+        for w in wr:
+            if w in wrote and wrote[w][0] != own:
+                toks.append(wrote[w])
+            toks += [t for t in read.get(w, []) if t[0] != own]
+        wait(q, toks)
+
+    def after(tok, rd, wr):
+        for r in rd:
+            read.setdefault(r, []).append(tok)
+        for w in wr:
+            wrote[w] = tok
+            read[w] = []
+
+    def op(q, rd, wr, f):
+        before(q, rd, wr)
+        s = "e" + q
+        f(queue[q]).then_inc(T.sem[s], 1)
+        total[s] = total.get(s, 0) + 1
+        after((s, total[s]), rd, wr)
+
+    def dma(q, rd, wr, out, in_):
+        before(q, rd, wr)
+        s = "d%d" % ndma[0]
+        ndma[0] += 1
+        queue[q].dma_start(out, in_).then_inc(T.sem[s], 16)
+        after((s, 16), rd, wr)
+        return (s, 16)
+
+    def send(dst, rd, out, in_, rsem):
+        before("p", rd, [])
+        rid, pid = topo.addr(dst)[:2]
+        g.remote_dma(out, in_, T.sem[rsem], T.sem.sent, pid, rid, topo.mask(core, dst))
+        total["sent"] = total.get("sent", 0) + len(topo.engines(core, dst))
+
+    def tt(out, a, b, o, rd, wr):
+        op("v", rd, wr, lambda e: e.tensor_tensor(out, a, b, o))
+
+    def ts(out, a, s1, o1, rd, wr, s2=None, o2=None):
+        if o2 is None:
+            op("v", rd, wr, lambda e: e.tensor_scalar(out, a, s1, None, o1))
+        else:
+            op("v", rd, wr, lambda e: e.tensor_scalar(out, a, s1, s2, o1, o2))
+
+    def cp(q, out, a, rd, wr, scale=None):
+        if q == "v":
+            op("v", rd, wr, lambda e: e.tensor_copy(out, a))
+        elif scale is None:
+            op("s", rd, wr, lambda e: e.activation(out, a, COPY))
+        else:
+            op("s", rd, wr, lambda e: e.activation(out, a, COPY, scale=scale))
+
+    def gather(q, out, win, lst):
+        cp(q, T[out][:, :], T[win][:, :].indirect(T[lst][:, 0:L]), [win, lst], [out])
+
+    def scatter(out, lst, src):
+        op("v", [src, lst], [out], lambda e: e.tensor_copy(T[out][:, :].indirect(T[lst][:, 0:L]), T[src][:, :]))
+
+    def scan(src, tmp):
+        op("v", [src, "md"], [tmp], lambda e: e.tensor_tensor_scan(T[tmp][:, :], T.md[:, 0:C], T[src][:, :], 0.0, MUL, ADD))
+
+    def wrapped(out, tmp, wr):
+        ts(out, T[tmp][:, 15:C:16], T.fac[:, :], MUL, [tmp, "fac"], wr, 192.0, ADD)
+
+    def quant(qn, sn, xn, h, rd):
+        a, b = HALF * h, HALF * h + HALF
+        op("v", rd, ["%s:%d" % (qn, h)], lambda e: e.quantize_mx(T[qn][:, a:b], T[sn][:, a:b], T[xn][:, 4 * a:4 * b]))
+
+    def mm(bank, w, ws, x, xs, lo, hi, rd):
+        op("t", rd, ["ps%d" % bank], lambda e: e.matmul_mx(T["ps%d" % bank][:, 0:hi - lo], w, ws, T[x][:, lo:hi], T[xs][:, lo:hi], True, True))
+
+    def block(q, b):
+        return T[q][:, 128 * b:128 * b + 128]
+
+    dma("s", [], ["xt0"], T.xt0[:, :], T.x[:, :])
+    dma("y", [], ["cin"], T.cin[:, :], T.cl[:, :])
+    dma("y", [], ["minp"], T.minp[:, :], T.ml[:, :])
+    dma("y", [], ["pin"], T.pin[:, :], T.pl[:, :])
+    dma("y", [], ["uin"], T.uin[:, :], T.u[:, :])
+    wait("y", [wrote["xt0"]])
+    dma("y", [], ["wcb"], T.wcb[:, :].bitcast(dt.uint8), T.wc[:, :])
+    dma("y", [], ["wsb"], T.wsb[:, :], T.ws[:, :])
+    dma("y", [], ["vin"], T.vin[:, :], T.v[:, :])
+
+    op("p", [], ["r16"], lambda e: e.iota(T.r16[:, :], [[1, 16]], 128, -1))
+    op("p", [], ["pcol"], lambda e: e.iota(T.pcol[:, :], [[0, 1]], 0, 1))
+    op("v", [], ["ones"], lambda e: e.memset(T.ones[:, :], 1.0))
+    op("p", ["ones"], ["diag"], lambda e: e.affine_select(T.diag[:, :], T.ones[:, :], [[-1, 128]], EQ, 0.0, 0, 1))
+    op("p", [], ["iob"], lambda e: e.iota(T.iob[:, :], [[1, C]], -192, 0, allow_small_or_imprecise_dtypes=True))
+    op("p", [], ["q24"], lambda e: e.iota(T.q24[:, :], [[16, L]], 0, 0, allow_small_or_imprecise_dtypes=True))
+    op("p", [], ["uli"], lambda e: e.iota(T.uli[:, :], [[16, 8]], 0, 0))
+    op("v", [], ["eb"], lambda e: e.memset(T.eb[:, :], 0.0))
+    ts(T.r15[:, :], T.r16[:, :], 15, AND, ["r16"], ["r15"])
+    ts(T.p15[:, :], T.pcol[:, :], 15, AND, ["pcol"], ["p15"])
+    ts(T.mda[:, :], T.r15[:, :], 1.0, EQ, ["r15"], ["mda"], BIG, MUL)
+    ts(T.mdb[:, :], T.r15[:, :], 0.0, NE, ["r15"], ["mdb"])
+    ts(T.fac[:, :], T.p15[:, :], 15.0, EQ, ["p15"], ["fac"], 1.0 / BIG, MAX)
+    ts(T.thr[:, :], T.p15[:, :], 15.0, NE, ["p15"], ["thr"], 2.0 ** 20, MUL)
+    cp("v", T.p15f[:, :], T.p15[:, :], ["p15"], ["p15f"])
+    tt(T.md[:, 0:16], T.mda[:, :], T.mdb[:, :], MAX, ["mda", "mdb"], ["md"])
+    for b in range(4):
+        cp("v", T.eb[:, 512 * b + b:512 * b + 512:4], T.diag[:, :], ["diag", "eb"], ["eb%d" % b])
+    k = 16
+    while k < 2 * C:
+        w = min(k, 2 * C - k)
+        cp("v", T.md[:, k:k + w], T.md[:, 0:w], ["md"], ["md"])
+        k += w
+    op("v", ["eb%d" % b for b in range(4)], ["qe"], lambda e: e.quantize_mx(T.qe[:, :], T.se[:, :], T.eb[:, :]))
+    ts(T.base[:, 0:L], T.q24[:, :], T.p15f[:, :], ADD, ["q24", "p15f"], ["base0"])
+    cp("v", T.ul[:, :], T.uli[:, :], ["uli"], ["ul"])
+
+    cp("v", T.cu[:, :], T.cin[:, :], ["cin"], ["cu"])
+    scatter("cib", "cu", "iob")
+    cp("v", T.mu[:, :], T.minp[:, :], ["minp"], ["mu"])
+    cp("v", T.au[:, :], T.pin[:, :], ["pin"], ["au"])
+    gather("s", "cb", "iob", "cu")
+    gather("s", "mb", "iob", "mu")
+    gather("s", "cmb", "cb", "mu")
+    scan("cib", "sc0")
+    wrapped(T.ciu[:, :], "sc0", ["ciu"])
+    wrapped(T.base[:, L:2 * L], "sc0", ["base1"])
+    gather("s", "hb", "cmb", "ciu")
+    gather("s", "fb", "mb", "ciu")
+    gather("s", "aib", "iob", "au")
+    gather("s", "acb", "aib", "ciu")
+
+    def tables():
+        rd = ["base0", "base1", "alt0", "alt1"]
+        tt(T.mx[:, :], T.base[:, :], T.alt[:, :], MAX, rd, ["mx"])
+        tt(T.mn[:, :], T.base[:, :], T.alt[:, :], MIN, rd, ["mn"])
+        cp("v", T.hiu[:, :], T.mx[:, :], ["mx"], ["hiu"])
+        cp("v", T.lou[:, :], T.mn[:, :], ["mn"], ["lou"])
+        tt(T.lt[:, :], T.base[:, :], T.alt[:, :], LT, rd, ["lt"])
+        tt(T.dd[:, :], T.alt[:, :], T.base[:, :], SUB, rd, ["dd"])
+
+    def state(d):
+        for h in range(2):
+            quant("qx%d" % d, "sx%d" % d, "xt%d" % d, h, ["xt0"] if d == 0 else ["xt%d:%d" % (d, b) for b in range(4)])
+
+    stores = []
+    for d in range(ROUNDS):
+        last = d == ROUNDS - 1
+        to = T.cores[(rank + d + 1) % n]
+        q, sx, lc, ls = "qx%d" % d, "sx%d" % d, "lc%d" % d, "ls%d" % d
+        la, lk, off, ku = "la%d" % d, "lk%d" % d, "off%d" % d, "ku%d" % d
+        qq = [q + ":0", q + ":1"]
+        state(d)
+        send(to, qq, T[lc][:, :].bitcast(dt.uint8), T[q][:, :].bitcast(dt.uint8), "ac%d" % d)
+        send(to, qq, T[ls][:, :], T[sx][:, :], "ac%d" % d)
+        nl = len(topo.engines(core, to))
+        wrote[lc], wrote[la], wrote[lk] = ("ac%d" % d, 2 * nl), ("aa%d" % d, nl), ("ak%d" % d, nl)
+        if d == 0:
+            op("v", ["uin"], ["qu0"], lambda e: e.quantize_mx(T.qu0[:, :], T.su0[:, :], T.uin[:, :]))
+            op("v", ["qu0", "ul"], ["qu"], lambda e: e.tensor_copy(T.qu[:, :].bitcast(dt.uint32), T.qu0[:, :].bitcast(dt.uint32).indirect(T.ul[:, :])))
+            op("v", ["qu0", "ul"], ["su"], lambda e: e.tensor_copy(T.su[:, :], T.su0[:, :].indirect(T.ul[:, :])))
+        for h in range(2):
+            mm(h, T.qu[:, :], T.su[:, :], q, sx, HALF * h, HALF * h + HALF, ["qu", "su", qq[h]])
+        for b in range(4):
+            mm(2 + b, block("qe", b), block("se", b), q, sx, 0, C, ["qe"] + qq)
+        if d == 0:
+            scan("hb", "sc1")
+            wrapped(T.alt[:, 0:L], "sc1", ["alt0"])
+            scan("fb", "sc2")
+            wrapped(T.alt[:, L:2 * L], "sc2", ["alt1"])
+            tables()
+        cp("v", T.sw[:, 0:HALF], T.ps0[:, 0:HALF], ["ps0"], ["sw0"])
+        cp("s", T.sw[:, HALF:C], T.ps1[:, 0:HALF], ["ps1"], ["sw1"])
+        sw, s2 = T.sw[:, :], ["sw0", "sw1"]
+        if d == 0:
+            cp("s", T.gg[:, 0:C], sw.indirect(T.hiu[:, 0:L]), s2 + ["hiu"], ["gg0", "gg1"])
+            scatter("bb", "au", "cb")
+        else:
+            cp("s", T.gg[:, 0:HALF], sw.indirect(T.hiu[:, 0:L // 2]), s2 + ["hiu"], ["gg0"])
+            cp("v", T.gg[:, HALF:C], sw.indirect(T.hiu[:, L // 2:L]), s2 + ["hiu"], ["gg1"])
+        cp("s", T.gg[:, C:2 * C], sw.indirect(T.hiu[:, L:2 * L]), s2 + ["hiu"], ["gg2"])
+        tt(T.ab[:, 0:C], sw.indirect(T.lou[:, 0:L]), T.gg[:, 0:C], GE, s2 + ["lou", "gg0", "gg1"], ["ab0"])
+        if d == 0:
+            scan("acb", "sc0")
+            wrapped(T.acu[:, :], "sc0", ["acu"])
+            gather("s", "bmb", "bb", "mu")
+            gather("s", "n0b", "bmb", "acu")
+        tt(T.ab[:, C:2 * C], sw.indirect(T.lou[:, L:2 * L]), T.gg[:, C:2 * C], GE, s2 + ["lou", "gg2"], ["ab1"])
+        op("v", ["ab0", "ab1", "md"], ["scab"], lambda e: e.tensor_tensor_scan(T.scab[:, :], T.md[:, :], T.ab[:, :], 0.0, MUL, ADD))
+        ts(T.bits[:, :], T.scab[:, 15:2 * C:16], T.thr[:, :], GT, ["scab", "thr"], ["bits"])
+        tt(T.abv[:, :], T.bits[:, :], T.lt[:, :], EQ, ["bits", "lt"], ["abv"])
+        tt(T.unl[:, 0:L], T.abv[:, 0:L], T.abv[:, L:2 * L], NE, ["abv"], ["unl0"])
+        tt(T.unl[:, L:2 * L], T.abv[:, 0:L], T.abv[:, L:2 * L], NE, ["abv"], ["unl1"])
+        tt(T.pr[:, :], T.unl[:, :], T.dd[:, :], MUL, ["unl0", "unl1", "dd"], ["pr"])
+        tt(T.rr[:, :], T.base[:, :], T.pr[:, :], ADD, ["base0", "base1", "pr"], ["rr"])
+        cp("v", T[off][:, :], T.rr[:, :], ["rr"], [off])
+        send(to, [off], T[la][:, :], T[off][:, L:2 * L], "aa%d" % d)
+        gather("s", "shb", "iob", off)
+        gather("v", "wb", "n0b", off)
+        scan("wb", "sc0")
+        wrapped(T.wu[:, :], "sc0", ["wu"])
+        gather("v", "kb", "shb", "wu")
+        scan("kb", "sc1")
+        wrapped(T[ku][:, :], "sc1", [ku])
+        send(to, [ku], T[lk][:, :], T[ku][:, :], "ak%d" % d)
+        bank = [6, 7, 0, 1]
+        for b in range(4):
+            mm(bank[b], block("qe", b), block("se", b), lc, ls, 0, C, ["qe", lc])
+        if not last:
+            gather("s", "alb", "shb", "ciu")
+            gather("s", "gab", "cb", off)
+            gather("s", "fb", "kb", "ciu")
+            scan("fb", "sc2")
+            wrapped(T.fu[:, :], "sc2", ["fu"])
+            wrapped(T.alt[:, L:2 * L], "sc2", ["alt1"])
+            gather("v", "hb", "cb", "fu")
+            scan("alb", "sc1")
+            wrapped(T.alu[:, :], "sc1", ["alu"])
+            scan("hb", "sc0")
+            wrapped(T.alt[:, 0:L], "sc0", ["alt0"])
+        else:
+            ts(T.cof[:, :], T.kb[:, :], 192.0, ADD, ["kb"], ["cof"])
+            stores.append(("y", dma("y", ["cof"], [], T.co[:, :], T.cof[0:128:16, :])))
+            op("v", ["vin"], ["qv"], lambda e: e.quantize_mx(T.qv[:, :], T.sv[:, :], T.vin[:, :]))
+        for b in range(4):
+            cp("s", T.tp[:, C * b:C * b + C], T["ps%d" % bank[b]][:, 0:C], ["ps%d" % bank[b]], ["tp%d" % b], 0.5)
+        for b in range(4):
+            s = slice(C * b, C * b + C)
+            cp("s", T.gb[:, s], T.tp[:, s].indirect(T[la][:, :]), ["tp%d" % b, la], ["gb%d" % b])
+            tt(T.zt[:, b:4 * C:4], T.tp[:, s].indirect(T[lk][:, :]), T.gb[:, s], ADD, ["tp%d" % b, lk, "gb%d" % b], ["zt%d" % b])
+        for h in range(2):
+            quant("qz", "sz", "zt", h, ["zt%d" % b for b in range(4)])
+        if not last:
+            gather("s", "alb", "hb", "alu")
+            scan("alb", "sc2")
+            wrapped(T.beu[:, :], "sc2", ["beu"])
+            tables()
+        for b in range(4):
+            s = slice(C * b, C * b + C)
+            for t in {0: (0, 1, 2), 2: (3,)}.get(b, ()):
+                cp("s", T.tb[:, C * t:C * t + C], T["ps%d" % (2 + t)][:, 0:C], ["ps%d" % (2 + t)], ["tb%d" % t])
+            for h in range(2):
+                k = (2 * b + h + 6) % 8
+                a = C * b + HALF * h
+                mm(k, block("wcb", b), block("wsb", b), "qz", "sz", HALF * h, HALF * h + HALF, ["wcb", "wsb", "qz:%d" % h])
+                cp("s", T.rs[:, a:a + HALF], T["ps%d" % k][:, 0:HALF], ["ps%d" % k], ["rs%d:%d" % (b, h)], 0.03125)
+            tt(T["xt%d" % (d + 1)][:, b:4 * C:4], T.rs[:, s].indirect(T[off][:, L:2 * L]), T.tb[:, s], ADD,
+               ["rs%d:0" % b, "rs%d:1" % b, off, "tb%d" % b], ["xt%d:%d" % (d + 1, b)])
+        if not last:
+            gather("s", "n0b", "gab", "beu")
+
+    d = ROUNDS
+    state(d)
+    q, sx = "qx%d" % d, "sx%d" % d
+    qq = [q + ":0", q + ":1"]
+    for h in range(2):
+        mm(h, T.qv[:, :], T.sv[:, :], q, sx, HALF * h, HALF * h + HALF, ["qv", qq[h]])
+    stores.append(("y", dma("y", qq, [], T.oc[:, :], T[q][:, :].bitcast(dt.uint8))))
+    for i in range(4):
+        stores.append(("y", dma("y", qq, [], T.osc[4 * i:4 * i + 4, :], T[sx][32 * i:32 * i + 4, :])))
+    cp("v", T.yb[:, 0:HALF], T.ps0[:, 0:HALF], ["ps0"], ["yb0"])
+    cp("s", T.yb[:, HALF:C], T.ps1[:, 0:HALF], ["ps1"], ["yb1"])
+    stores.append(("y", dma("y", ["yb0"], [], T.y[:, 0:HALF], T.yb[:, 0:HALF])))
+    stores.append(("s", dma("s", ["yb1"], [], T.y[:, HALF:C], T.yb[:, HALF:C])))
+    for q, tok in stores:
+        wait(q, [tok])
+    wait("p", [(s, total[s]) for s in ("ev", "es", "et", "ep", "sent")])

@@ -3,23 +3,24 @@ from concourse.mybir import dt, AluOpType, ActivationFunctionType
 C = 384
 L = 24
 HALF = C // 2
+FIRST = 128
 ROUNDS = 3
 BIG = 2.0 ** 40
 
 SCRATCH = {
     "uin": ("sbuf", [128, 512], "bfloat16"), "vin": ("sbuf", [128, 512], "bfloat16"),
     "wcb": ("sbuf", [128, 512], "float8_e4m3fn_x4"), "wsb": ("sbuf", [128, 512], "uint8"),
-    "ones": ("sbuf", [128, 128], "bfloat16"), "diag": ("sbuf", [128, 128], "bfloat16"),
+    "ones": ("sbuf", [128, 512], "bfloat16"),
     "eb": ("sbuf", [128, 2048], "bfloat16"), "qe": ("sbuf", [128, 512], "float8_e4m3fn_x4"), "se": ("sbuf", [128, 512], "uint8"),
-    "r16": ("sbuf", [128, 16], "int32"), "r15": ("sbuf", [128, 16], "int32"),
-    "mda": ("sbuf", [128, 16], "bfloat16"), "mdb": ("sbuf", [128, 16], "bfloat16"), "md": ("sbuf", [128, 2 * C], "bfloat16"),
+    "r16": ("sbuf", [128, 16], "int32"), "r15": ("sbuf", [128, 16], "int32"), "md": ("sbuf", [128, 2 * C], "bfloat16"),
+    "mda": ("sbuf", [128, 16], "bfloat16"), "mdb": ("sbuf", [128, 16], "bfloat16"), "mdc": ("sbuf", [128, 16], "bfloat16"),
     "pcol": ("sbuf", [128, 1], "int32"), "p15": ("sbuf", [128, 1], "int32"), "p15f": ("sbuf", [128, 1], "float32"),
-    "fac": ("sbuf", [128, 1], "float32"), "thr": ("sbuf", [128, 1], "float32"),
+    "fac": ("sbuf", [128, 1], "float32"), "fsq": ("sbuf", [128, 1], "float32"), "nsq": ("sbuf", [128, 1], "float32"),
     "q24": ("sbuf", [128, L], "float32"), "uli": ("sbuf", [128, 8], "int32"), "ul": ("sbuf", [128, 8], "uint16"),
     "scab": ("sbuf", [128, 2 * C], "bfloat16"), "ab": ("sbuf", [128, 2 * C], "bfloat16"),
     "lou": ("sbuf", [128, 2 * L], "uint16"), "hiu": ("sbuf", [128, 2 * L], "uint16"),
     "sw": ("sbuf", [128, C], "float32"), "gg": ("sbuf", [128, 2 * C], "float32"),
-    "tb": ("sbuf", [128, 4 * C], "bfloat16"), "tp": ("sbuf", [128, 4 * C], "bfloat16"),
+    "tb": ("sbuf", [128, 4 * C], "bfloat16"), "tp": ("sbuf", [128, 4 * C], "bfloat16"), "tob": ("sbuf", [128, 4 * C], "bfloat16"),
     "gb": ("sbuf", [128, 4 * C], "bfloat16"), "zt": ("sbuf", [128, 4 * C], "bfloat16"),
     "qz": ("sbuf", [128, C], "float8_e4m3fn_x4"), "sz": ("sbuf", [128, C], "uint8"),
     "rs": ("sbuf", [128, 4 * C], "float32"), "cof": ("sbuf", [128, C], "float32"), "yb": ("sbuf", [128, C], "float32"),
@@ -30,11 +31,11 @@ for _k in ("su0", "su", "sv"):
     SCRATCH[_k] = ("sbuf", [128, 128], "uint8")
 for _k in ("cin", "minp", "pin"):
     SCRATCH[_k] = ("sbuf", [128, L], "int32")
-for _k in ("cu", "mu", "au", "ciu", "acu", "fu", "alu", "beu", "wu"):
+for _k in ("cu", "mu", "au", "ciu", "acu", "fu", "alu", "beu", "wu", "ou"):
     SCRATCH[_k] = ("sbuf", [128, L], "uint16")
-for _k in ("iob", "cb", "mb", "cmb", "cib", "aib", "acb", "bb", "bmb", "fb", "hb", "n0b", "shb", "alb", "gab", "wb", "kb", "sc0", "sc1", "sc2"):
+for _k in ("iob", "cb", "mb", "bb", "bmb", "fb", "hb", "n0b", "shb", "alb", "gab", "wb", "kb", "ob", "sc0", "sc1", "sc2"):
     SCRATCH[_k] = ("sbuf", [128, C], "bfloat16")
-for _k in ("base", "alt", "mn", "mx", "lt", "dd", "bits", "abv", "unl", "pr", "rr"):
+for _k in ("base", "alt", "mn", "mx", "lt", "dd", "yy", "yd", "sf", "dp", "p0", "sq", "pr", "rr"):
     SCRATCH[_k] = ("sbuf", [128, 2 * L], "float32")
 for _d in range(ROUNDS + 1):
     SCRATCH["xt%d" % _d] = ("sbuf", [128, 4 * C], "bfloat16")
@@ -54,7 +55,7 @@ SEMAPHORES = ["ev", "es", "et", "ep", "sent"] + ["d%d" % _k for _k in range(18)]
 SEMAPHORES += ["%s%d" % (_k, _d) for _d in range(ROUNDS) for _k in ("ac", "aa", "ak")]
 
 ADD, SUB, MUL, MIN, MAX = AluOpType.add, AluOpType.subtract, AluOpType.mult, AluOpType.min, AluOpType.max
-GE, GT, LT, EQ, NE = AluOpType.is_ge, AluOpType.is_gt, AluOpType.is_lt, AluOpType.is_equal, AluOpType.not_equal
+GE, LT, EQ, NE = AluOpType.is_ge, AluOpType.is_lt, AluOpType.is_equal, AluOpType.not_equal
 AND = AluOpType.bitwise_and
 COPY = ActivationFunctionType.Copy
 
@@ -78,12 +79,10 @@ def rank_program(g, core, T, topo):
                 seen[(q, s)] = need[s]
 
     def before(q, rd, wr):
-        own = "e" + q
         toks = [wrote[r] for r in rd if r in wrote]
         for w in wr:
-            if w in wrote and wrote[w][0] != own:
-                toks.append(wrote[w])
-            toks += [t for t in read.get(w, []) if t[0] != own]
+            toks += [wrote[w]] if w in wrote else []
+            toks += read.get(w, [])
         wait(q, toks)
 
     def after(tok, rd, wr):
@@ -106,7 +105,7 @@ def rank_program(g, core, T, topo):
         ndma[0] += 1
         queue[q].dma_start(out, in_).then_inc(T.sem[s], 16)
         after((s, 16), rd, wr)
-        return (s, 16)
+        return q, (s, 16)
 
     def send(dst, rd, out, in_, rsem):
         before("p", rd, [])
@@ -138,13 +137,12 @@ def rank_program(g, core, T, topo):
         op("v", [src, lst], [out], lambda e: e.tensor_copy(T[out][:, :].indirect(T[lst][:, 0:L]), T[src][:, :]))
 
     def scan(src, tmp):
-        op("v", [src, "md"], [tmp], lambda e: e.tensor_tensor_scan(T[tmp][:, :], T.md[:, 0:C], T[src][:, :], 0.0, MUL, ADD))
+        op("v", [src, "md"], [tmp], lambda e: e.tensor_tensor_scan(T[tmp][:, :], T.md[:, 0:2 * C:2], T[src][:, :], 0.0, MUL, ADD))
 
     def wrapped(out, tmp, wr):
         ts(out, T[tmp][:, 15:C:16], T.fac[:, :], MUL, [tmp, "fac"], wr, 192.0, ADD)
 
-    def quant(qn, sn, xn, h, rd):
-        a, b = HALF * h, HALF * h + HALF
+    def quant(qn, sn, xn, h, a, b, rd):
         op("v", rd, ["%s:%d" % (qn, h)], lambda e: e.quantize_mx(T[qn][:, a:b], T[sn][:, a:b], T[xn][:, 4 * a:4 * b]))
 
     def mm(bank, w, ws, x, xs, lo, hi, rd):
@@ -153,12 +151,13 @@ def rank_program(g, core, T, topo):
     def block(q, b):
         return T[q][:, 128 * b:128 * b + 128]
 
-    dma("s", [], ["xt0"], T.xt0[:, :], T.x[:, :])
-    dma("y", [], ["cin"], T.cin[:, :], T.cl[:, :])
+    dma("y", [], ["xt0a"], T.xt0[:, 0:4 * FIRST], T.x[:, 0:4 * FIRST])
+    dma("s", [], ["cin"], T.cin[:, :], T.cl[:, :])
     dma("y", [], ["minp"], T.minp[:, :], T.ml[:, :])
-    dma("y", [], ["pin"], T.pin[:, :], T.pl[:, :])
+    dma("s", [], ["pin"], T.pin[:, :], T.pl[:, :])
+    dma("y", [], ["xt0b"], T.xt0[:, 4 * FIRST:4 * C], T.x[:, 4 * FIRST:4 * C])
     dma("y", [], ["uin"], T.uin[:, :], T.u[:, :])
-    wait("y", [wrote["xt0"]])
+    wait("y", [wrote["xt0b"]])
     dma("y", [], ["wcb"], T.wcb[:, :].bitcast(dt.uint8), T.wc[:, :])
     dma("y", [], ["wsb"], T.wsb[:, :], T.ws[:, :])
     dma("y", [], ["vin"], T.vin[:, :], T.v[:, :])
@@ -166,114 +165,143 @@ def rank_program(g, core, T, topo):
     op("p", [], ["r16"], lambda e: e.iota(T.r16[:, :], [[1, 16]], 128, -1))
     op("p", [], ["pcol"], lambda e: e.iota(T.pcol[:, :], [[0, 1]], 0, 1))
     op("v", [], ["ones"], lambda e: e.memset(T.ones[:, :], 1.0))
-    op("p", ["ones"], ["diag"], lambda e: e.affine_select(T.diag[:, :], T.ones[:, :], [[-1, 128]], EQ, 0.0, 0, 1))
+    op("p", ["ones"], ["eb0"], lambda e: e.affine_select(T.eb[:, 0:512], T.ones[:, :], [[-1, 128], [1000, 4]], EQ, 0.0, 0, 1))
     op("p", [], ["iob"], lambda e: e.iota(T.iob[:, :], [[1, C]], -192, 0, allow_small_or_imprecise_dtypes=True))
     op("p", [], ["q24"], lambda e: e.iota(T.q24[:, :], [[16, L]], 0, 0, allow_small_or_imprecise_dtypes=True))
     op("p", [], ["uli"], lambda e: e.iota(T.uli[:, :], [[16, 8]], 0, 0))
-    op("v", [], ["eb"], lambda e: e.memset(T.eb[:, :], 0.0))
+    for b in range(1, 4):
+        a = 512 * b
+        cp("s", T.eb[:, a + b:a + 512], T.eb[:, 0:512 - b], ["eb0"], ["eb%d" % b])
+        cp("s", T.eb[:, a:a + b], T.eb[:, 512 - b:512], ["eb0"], ["eb%d:0" % b])
     ts(T.r15[:, :], T.r16[:, :], 15, AND, ["r16"], ["r15"])
     ts(T.p15[:, :], T.pcol[:, :], 15, AND, ["pcol"], ["p15"])
     ts(T.mda[:, :], T.r15[:, :], 1.0, EQ, ["r15"], ["mda"], BIG, MUL)
     ts(T.mdb[:, :], T.r15[:, :], 0.0, NE, ["r15"], ["mdb"])
     ts(T.fac[:, :], T.p15[:, :], 15.0, EQ, ["p15"], ["fac"], 1.0 / BIG, MAX)
-    ts(T.thr[:, :], T.p15[:, :], 15.0, NE, ["p15"], ["thr"], 2.0 ** 20, MUL)
+    tt(T.md[:, 0:32:2], T.mda[:, :], T.mdb[:, :], MAX, ["mda", "mdb"], ["md"])
+    ts(T.mdc[:, :], T.mdb[:, :], 2.0, MUL, ["mdb"], ["mdc"])
     cp("v", T.p15f[:, :], T.p15[:, :], ["p15"], ["p15f"])
-    tt(T.md[:, 0:16], T.mda[:, :], T.mdb[:, :], MAX, ["mda", "mdb"], ["md"])
-    for b in range(4):
-        cp("v", T.eb[:, 512 * b + b:512 * b + 512:4], T.diag[:, :], ["diag", "eb"], ["eb%d" % b])
-    k = 16
+    tt(T.fsq[:, :], T.fac[:, :], T.fac[:, :], MUL, ["fac"], ["fsq"])
+    ts(T.md[:, 1:32:2], T.mdc[:, :], -1.0, ADD, ["mdc"], ["md1"])
+    ts(T.nsq[:, :], T.fsq[:, :], -2.0, MUL, ["fsq"], ["nsq"])
+    k = 32
     while k < 2 * C:
         w = min(k, 2 * C - k)
-        cp("v", T.md[:, k:k + w], T.md[:, 0:w], ["md"], ["md"])
+        cp("v", T.md[:, k:k + w], T.md[:, 0:w], ["md", "md1"], ["md"])
         k += w
-    op("v", ["eb%d" % b for b in range(4)], ["qe"], lambda e: e.quantize_mx(T.qe[:, :], T.se[:, :], T.eb[:, :]))
     ts(T.base[:, 0:L], T.q24[:, :], T.p15f[:, :], ADD, ["q24", "p15f"], ["base0"])
     cp("v", T.ul[:, :], T.uli[:, :], ["uli"], ["ul"])
 
     cp("v", T.cu[:, :], T.cin[:, :], ["cin"], ["cu"])
-    scatter("cib", "cu", "iob")
-    cp("v", T.mu[:, :], T.minp[:, :], ["minp"], ["mu"])
-    cp("v", T.au[:, :], T.pin[:, :], ["pin"], ["au"])
+    quant("qx0", "sx0", "xt0", 0, 0, FIRST, ["xt0a"])
+    send(T.cores[(rank + 1) % n], ["qx0:0"], T.lc0[:, 0:FIRST].bitcast(dt.uint8), T.qx0[:, 0:FIRST].bitcast(dt.uint8), "ac0")
     gather("s", "cb", "iob", "cu")
+    cp("v", T.mu[:, :], T.minp[:, :], ["minp"], ["mu"])
+    scatter("alb", "cu", "iob")
+    gather("s", "gab", "cb", "mu")
     gather("s", "mb", "iob", "mu")
-    gather("s", "cmb", "cb", "mu")
-    scan("cib", "sc0")
+    cp("v", T.au[:, :], T.pin[:, :], ["pin"], ["au"])
+    scan("alb", "sc0")
     wrapped(T.ciu[:, :], "sc0", ["ciu"])
     wrapped(T.base[:, L:2 * L], "sc0", ["base1"])
-    gather("s", "hb", "cmb", "ciu")
+    quant("qx0", "sx0", "xt0", 1, FIRST, C, ["xt0b"])
+    gather("s", "hb", "gab", "ciu")
     gather("s", "fb", "mb", "ciu")
-    gather("s", "aib", "iob", "au")
-    gather("s", "acb", "aib", "ciu")
+    scatter("bb", "au", "cb")
 
-    def tables():
+    def tables(part):
         rd = ["base0", "base1", "alt0", "alt1"]
-        tt(T.mx[:, :], T.base[:, :], T.alt[:, :], MAX, rd, ["mx"])
-        tt(T.mn[:, :], T.base[:, :], T.alt[:, :], MIN, rd, ["mn"])
-        cp("v", T.hiu[:, :], T.mx[:, :], ["mx"], ["hiu"])
-        cp("v", T.lou[:, :], T.mn[:, :], ["mn"], ["lou"])
-        tt(T.lt[:, :], T.base[:, :], T.alt[:, :], LT, rd, ["lt"])
-        tt(T.dd[:, :], T.alt[:, :], T.base[:, :], SUB, rd, ["dd"])
+        if part == 0:
+            tt(T.mx[:, :], T.base[:, :], T.alt[:, :], MAX, rd, ["mx"])
+            tt(T.mn[:, :], T.base[:, :], T.alt[:, :], MIN, rd, ["mn"])
+            cp("v", T.hiu[:, :], T.mx[:, :], ["mx"], ["hiu"])
+            cp("v", T.lou[:, :], T.mn[:, :], ["mn"], ["lou"])
+        elif part == 1:
+            tt(T.lt[:, :], T.base[:, :], T.alt[:, :], LT, rd, ["lt"])
+            tt(T.dd[:, :], T.alt[:, :], T.base[:, :], SUB, rd, ["dd"])
+        elif part == 2:
+            tt(T.yy[:, 0:L], T.lt[:, 0:L], T.lt[:, L:2 * L], NE, ["lt"], ["yy0"])
+            tt(T.yy[:, L:2 * L], T.lt[:, 0:L], T.lt[:, L:2 * L], NE, ["lt"], ["yy1"])
+        elif part == 3:
+            ts(T.sf[:, :], T.yy[:, :], T.nsq[:, :], MUL, ["yy0", "yy1", "nsq", "fsq"], ["sf"], T.fsq[:, :], ADD)
+            tt(T.yd[:, :], T.yy[:, :], T.dd[:, :], MUL, ["yy0", "yy1", "dd"], ["yd"])
+        else:
+            tt(T.dp[:, :], T.sf[:, :], T.dd[:, :], MUL, ["sf", "dd"], ["dp"])
+            tt(T.p0[:, :], T.base[:, :], T.yd[:, :], ADD, ["base0", "base1", "yd"], ["p0"])
 
     def state(d):
         for h in range(2):
-            quant("qx%d" % d, "sx%d" % d, "xt%d" % d, h, ["xt0"] if d == 0 else ["xt%d:%d" % (d, b) for b in range(4)])
+            quant("qx%d" % d, "sx%d" % d, "xt%d" % d, h, HALF * h, HALF * h + HALF, ["xt%d:%d" % (d, b) for b in range(4)])
 
     stores = []
     for d in range(ROUNDS):
         last = d == ROUNDS - 1
         to = T.cores[(rank + d + 1) % n]
-        q, sx, lc, ls = "qx%d" % d, "sx%d" % d, "lc%d" % d, "ls%d" % d
+        q, sx, lc, ls, x1 = "qx%d" % d, "sx%d" % d, "lc%d" % d, "ls%d" % d, "xt%d" % (d + 1)
         la, lk, off, ku = "la%d" % d, "lk%d" % d, "off%d" % d, "ku%d" % d
         qq = [q + ":0", q + ":1"]
-        state(d)
-        send(to, qq, T[lc][:, :].bitcast(dt.uint8), T[q][:, :].bitcast(dt.uint8), "ac%d" % d)
+        lo = 0 if d else FIRST
+        if d:
+            state(d)
+        send(to, qq, T[lc][:, lo:C].bitcast(dt.uint8), T[q][:, lo:C].bitcast(dt.uint8), "ac%d" % d)
         send(to, qq, T[ls][:, :], T[sx][:, :], "ac%d" % d)
         nl = len(topo.engines(core, to))
-        wrote[lc], wrote[la], wrote[lk] = ("ac%d" % d, 2 * nl), ("aa%d" % d, nl), ("ak%d" % d, nl)
+        wrote[lc], wrote[la], wrote[lk] = ("ac%d" % d, (2 if d else 3) * nl), ("aa%d" % d, nl), ("ak%d" % d, nl)
         if d == 0:
             op("v", ["uin"], ["qu0"], lambda e: e.quantize_mx(T.qu0[:, :], T.su0[:, :], T.uin[:, :]))
             op("v", ["qu0", "ul"], ["qu"], lambda e: e.tensor_copy(T.qu[:, :].bitcast(dt.uint32), T.qu0[:, :].bitcast(dt.uint32).indirect(T.ul[:, :])))
-            op("v", ["qu0", "ul"], ["su"], lambda e: e.tensor_copy(T.su[:, :], T.su0[:, :].indirect(T.ul[:, :])))
+            cp("s", T.su[:, :], T.su0[:, :].indirect(T.ul[:, :]), ["qu0", "ul"], ["su"])
+            gather("s", "ob", "iob", "au")
+            gather("s", "wb", "ob", "ciu")
         for h in range(2):
-            mm(h, T.qu[:, :], T.su[:, :], q, sx, HALF * h, HALF * h + HALF, ["qu", "su", qq[h]])
-        for b in range(4):
-            mm(2 + b, block("qe", b), block("se", b), q, sx, 0, C, ["qe"] + qq)
+            mm(h, T.qu[:, :], T.su[:, :], q, sx, HALF * h, HALF * h + HALF, ["qu", "su"] + (qq[h:h + 1] if d else qq))
         if d == 0:
             scan("hb", "sc1")
-            wrapped(T.alt[:, 0:L], "sc1", ["alt0"])
             scan("fb", "sc2")
+            wrapped(T.alt[:, 0:L], "sc1", ["alt0"])
             wrapped(T.alt[:, L:2 * L], "sc2", ["alt1"])
-            tables()
+            tables(0)
         cp("v", T.sw[:, 0:HALF], T.ps0[:, 0:HALF], ["ps0"], ["sw0"])
         cp("s", T.sw[:, HALF:C], T.ps1[:, 0:HALF], ["ps1"], ["sw1"])
+        tables(1)
         sw, s2 = T.sw[:, :], ["sw0", "sw1"]
         if d == 0:
             cp("s", T.gg[:, 0:C], sw.indirect(T.hiu[:, 0:L]), s2 + ["hiu"], ["gg0", "gg1"])
-            scatter("bb", "au", "cb")
+            op("v", ["eb0"] + ["eb%d%s" % (b, e) for b in (1, 2, 3) for e in ("", ":0")], ["qe"], lambda e: e.quantize_mx(T.qe[:, :], T.se[:, :], T.eb[:, :]))
         else:
             cp("s", T.gg[:, 0:HALF], sw.indirect(T.hiu[:, 0:L // 2]), s2 + ["hiu"], ["gg0"])
             cp("v", T.gg[:, HALF:C], sw.indirect(T.hiu[:, L // 2:L]), s2 + ["hiu"], ["gg1"])
         cp("s", T.gg[:, C:2 * C], sw.indirect(T.hiu[:, L:2 * L]), s2 + ["hiu"], ["gg2"])
-        tt(T.ab[:, 0:C], sw.indirect(T.lou[:, 0:L]), T.gg[:, 0:C], GE, s2 + ["lou", "gg0", "gg1"], ["ab0"])
+        for b in range(4):
+            mm(2 + b, block("qe", b), block("se", b), q, sx, 0, C, ["qe"] + qq)
+        tables(2)
+        tt(T.ab[:, 0:2 * C:2], sw.indirect(T.lou[:, 0:L]), T.gg[:, 0:C], GE, s2 + ["lou", "gg0", "gg1"], ["ab0"])
         if d == 0:
-            scan("acb", "sc0")
-            wrapped(T.acu[:, :], "sc0", ["acu"])
+            scan("wb", "sc0")
             gather("s", "bmb", "bb", "mu")
+        tt(T.ab[:, 1:2 * C:2], sw.indirect(T.lou[:, L:2 * L]), T.gg[:, C:2 * C], GE, s2 + ["lou", "gg2"], ["ab1"])
+        if d == 0:
+            wrapped(T.acu[:, :], "sc0", ["acu"])
             gather("s", "n0b", "bmb", "acu")
-        tt(T.ab[:, C:2 * C], sw.indirect(T.lou[:, L:2 * L]), T.gg[:, C:2 * C], GE, s2 + ["lou", "gg2"], ["ab1"])
+        else:
+            gather("s", "n0b", "gab", "beu")
+        tables(3)
         op("v", ["ab0", "ab1", "md"], ["scab"], lambda e: e.tensor_tensor_scan(T.scab[:, :], T.md[:, :], T.ab[:, :], 0.0, MUL, ADD))
-        ts(T.bits[:, :], T.scab[:, 15:2 * C:16], T.thr[:, :], GT, ["scab", "thr"], ["bits"])
-        tt(T.abv[:, :], T.bits[:, :], T.lt[:, :], EQ, ["bits", "lt"], ["abv"])
-        tt(T.unl[:, 0:L], T.abv[:, 0:L], T.abv[:, L:2 * L], NE, ["abv"], ["unl0"])
-        tt(T.unl[:, L:2 * L], T.abv[:, 0:L], T.abv[:, L:2 * L], NE, ["abv"], ["unl1"])
-        tt(T.pr[:, :], T.unl[:, :], T.dd[:, :], MUL, ["unl0", "unl1", "dd"], ["pr"])
-        tt(T.rr[:, :], T.base[:, :], T.pr[:, :], ADD, ["base0", "base1", "pr"], ["rr"])
+        tables(4)
+        w = T.scab[:, 31:2 * C:32]
+        tt(T.sq[:, 0:L], w, w, MUL, ["scab"], ["sq0"])
+        tt(T.sq[:, L:2 * L], w, w, MUL, ["scab"], ["sq1"])
+        tt(T.pr[:, :], T.sq[:, :], T.dp[:, :], MUL, ["sq0", "sq1", "dp"], ["pr"])
+        tt(T.rr[:, :], T.p0[:, :], T.pr[:, :], ADD, ["p0", "pr"], ["rr"])
         cp("v", T[off][:, :], T.rr[:, :], ["rr"], [off])
         send(to, [off], T[la][:, :], T[off][:, L:2 * L], "aa%d" % d)
+        for b in range(4):
+            cp("s", T.tb[:, C * b:C * b + C], T["ps%d" % (2 + b)][:, 0:C], ["ps%d" % (2 + b)], ["tb%d" % b])
         gather("s", "shb", "iob", off)
         gather("v", "wb", "n0b", off)
         scan("wb", "sc0")
         wrapped(T.wu[:, :], "sc0", ["wu"])
+        gather("s", "ob", "shb", "cu")
         gather("v", "kb", "shb", "wu")
         scan("kb", "sc1")
         wrapped(T[ku][:, :], "sc1", [ku])
@@ -281,62 +309,96 @@ def rank_program(g, core, T, topo):
         bank = [6, 7, 0, 1]
         for b in range(4):
             mm(bank[b], block("qe", b), block("se", b), lc, ls, 0, C, ["qe", lc])
+        scan("ob", "sc2")
         if not last:
             gather("s", "alb", "shb", "ciu")
-            gather("s", "gab", "cb", off)
             gather("s", "fb", "kb", "ciu")
-            scan("fb", "sc2")
-            wrapped(T.fu[:, :], "sc2", ["fu"])
-            wrapped(T.alt[:, L:2 * L], "sc2", ["alt1"])
+            scan("fb", "sc0")
+            wrapped(T.ou[:, :], "sc2", ["ou"])
+            wrapped(T.fu[:, :], "sc0", ["fu"])
+            wrapped(T.alt[:, L:2 * L], "sc0", ["alt1"])
             gather("v", "hb", "cb", "fu")
             scan("alb", "sc1")
+            scan("hb", "sc2")
             wrapped(T.alu[:, :], "sc1", ["alu"])
-            scan("hb", "sc0")
-            wrapped(T.alt[:, 0:L], "sc0", ["alt0"])
+            wrapped(T.alt[:, 0:L], "sc2", ["alt0"])
+            tables(0)
         else:
+            wrapped(T.ou[:, :], "sc2", ["ou"])
             ts(T.cof[:, :], T.kb[:, :], 192.0, ADD, ["kb"], ["cof"])
-            stores.append(("y", dma("y", ["cof"], [], T.co[:, :], T.cof[0:128:16, :])))
+            stores.append(dma("y", ["cof"], [], T.co[:, :], T.cof[0:128:16, :]))
             op("v", ["vin"], ["qv"], lambda e: e.quantize_mx(T.qv[:, :], T.sv[:, :], T.vin[:, :]))
-        for b in range(4):
+
+        def arrived(b):
             cp("s", T.tp[:, C * b:C * b + C], T["ps%d" % bank[b]][:, 0:C], ["ps%d" % bank[b]], ["tp%d" % b], 0.5)
+        arrived(0)
         for b in range(4):
             s = slice(C * b, C * b + C)
+            if b < 3:
+                arrived(b + 1)
             cp("s", T.gb[:, s], T.tp[:, s].indirect(T[la][:, :]), ["tp%d" % b, la], ["gb%d" % b])
             tt(T.zt[:, b:4 * C:4], T.tp[:, s].indirect(T[lk][:, :]), T.gb[:, s], ADD, ["tp%d" % b, lk, "gb%d" % b], ["zt%d" % b])
+        for b in (2, 3):
+            s = slice(C * b, C * b + C)
+            cp("s", T.tob[:, s], T.tb[:, s].indirect(T.ou[:, :]), ["tb%d" % b, "ou"], ["tob%d" % b], 32.0)
         for h in range(2):
-            quant("qz", "sz", "zt", h, ["zt%d" % b for b in range(4)])
+            quant("qz", "sz", "zt", h, HALF * h, HALF * h + HALF, ["zt%d" % b for b in range(4)])
         if not last:
             gather("s", "alb", "hb", "alu")
-            scan("alb", "sc2")
-            wrapped(T.beu[:, :], "sc2", ["beu"])
-            tables()
-        for b in range(4):
-            s = slice(C * b, C * b + C)
-            for t in {0: (0, 1, 2), 2: (3,)}.get(b, ()):
-                cp("s", T.tb[:, C * t:C * t + C], T["ps%d" % (2 + t)][:, 0:C], ["ps%d" % (2 + t)], ["tb%d" % t])
+        at = {}
+        for i, b in enumerate((2, 0, 3, 1)):
             for h in range(2):
-                k = (2 * b + h + 6) % 8
-                a = C * b + HALF * h
+                at[(b, h)] = k = (2 * i + h + 6) % 8
                 mm(k, block("wcb", b), block("wsb", b), "qz", "sz", HALF * h, HALF * h + HALF, ["wcb", "wsb", "qz:%d" % h])
-                cp("s", T.rs[:, a:a + HALF], T["ps%d" % k][:, 0:HALF], ["ps%d" % k], ["rs%d:%d" % (b, h)], 0.03125)
-            tt(T["xt%d" % (d + 1)][:, b:4 * C:4], T.rs[:, s].indirect(T[off][:, L:2 * L]), T.tb[:, s], ADD,
-               ["rs%d:0" % b, "rs%d:1" % b, off, "tb%d" % b], ["xt%d:%d" % (d + 1, b)])
+
+        def bring(b):
+            for h in range(2):
+                a, ps = C * b + HALF * h, "ps%d" % at[(b, h)]
+                if b < 2:
+                    cp("s", T.rs[:, a:a + HALF], T[ps][:, 0:HALF], [ps], ["rs%d:%d" % (b, h)], 0.03125)
+                else:
+                    tt(T.rs[:, a:a + HALF], T[ps][:, 0:HALF], T.tob[:, a:a + HALF], ADD, [ps, "tob%d" % b], ["rs%d:%d" % (b, h)])
+
+        def finish(b):
+            s = slice(C * b, C * b + C)
+            rd, wr = ["rs%d:0" % b, "rs%d:1" % b, off], ["%s:%d" % (x1, b)]
+            picked = T.rs[:, s].indirect(T[off][:, L:2 * L])
+            if b < 2:
+                tt(T[x1][:, b:4 * C:4], picked, T.tb[:, s], ADD, rd + ["tb%d" % b], wr)
+            else:
+                cp("s", T[x1][:, b:4 * C:4], picked, rd, wr, 0.03125)
+        bring(2)
+        bring(0)
         if not last:
-            gather("s", "n0b", "gab", "beu")
+            scan("alb", "sc1")
+            wrapped(T.beu[:, :], "sc1", ["beu"])
+        finish(0)
+        finish(2)
+        bring(1)
+        bring(3)
+        finish(1)
+        finish(3)
+        if not last:
+            gather("s", "gab", "cb", off)
 
     d = ROUNDS
     state(d)
     q, sx = "qx%d" % d, "sx%d" % d
     qq = [q + ":0", q + ":1"]
+
+    def scales(queue_name, i):
+        stores.append(dma(queue_name, qq, [], T.osc[4 * i:4 * i + 4, :], T[sx][32 * i:32 * i + 4, :]))
     for h in range(2):
         mm(h, T.qv[:, :], T.sv[:, :], q, sx, HALF * h, HALF * h + HALF, ["qv", qq[h]])
-    stores.append(("y", dma("y", qq, [], T.oc[:, :], T[q][:, :].bitcast(dt.uint8))))
-    for i in range(4):
-        stores.append(("y", dma("y", qq, [], T.osc[4 * i:4 * i + 4, :], T[sx][32 * i:32 * i + 4, :])))
+    stores.append(dma("y", qq, [], T.oc[:, :], T[q][:, :].bitcast(dt.uint8)))
+    scales("y", 0)
+    scales("y", 1)
     cp("v", T.yb[:, 0:HALF], T.ps0[:, 0:HALF], ["ps0"], ["yb0"])
     cp("s", T.yb[:, HALF:C], T.ps1[:, 0:HALF], ["ps1"], ["yb1"])
-    stores.append(("y", dma("y", ["yb0"], [], T.y[:, 0:HALF], T.yb[:, 0:HALF])))
-    stores.append(("s", dma("s", ["yb1"], [], T.y[:, HALF:C], T.yb[:, HALF:C])))
+    stores.append(dma("y", ["yb0"], [], T.y[:, 0:HALF], T.yb[:, 0:HALF]))
+    stores.append(dma("s", ["yb1"], [], T.y[:, HALF:C], T.yb[:, HALF:C]))
+    scales("s", 2)
+    scales("s", 3)
     for q, tok in stores:
         wait(q, [tok])
     wait("p", [(s, total[s]) for s in ("ev", "es", "et", "ep", "sent")])

from concourse.mybir import dt, AluOpType, ActivationFunctionType

C = 384
L = 24
HALF = C // 2
FIRST = 128
ROUNDS = 3
BIG = 2.0 ** 40

SCRATCH = {
    "uin": ("sbuf", [128, 512], "bfloat16"), "vin": ("sbuf", [128, 512], "bfloat16"),
    "wcb": ("sbuf", [128, 512], "float8_e4m3fn_x4"), "wsb": ("sbuf", [128, 512], "uint8"),
    "ones": ("sbuf", [128, 512], "bfloat16"),
    "eb": ("sbuf", [128, 2048], "bfloat16"), "qe": ("sbuf", [128, 512], "float8_e4m3fn_x4"), "se": ("sbuf", [128, 512], "uint8"),
    "r16": ("sbuf", [128, 16], "int32"), "r15": ("sbuf", [128, 16], "int32"), "md": ("sbuf", [128, 2 * C], "bfloat16"),
    "mda": ("sbuf", [128, 16], "bfloat16"), "mdb": ("sbuf", [128, 16], "bfloat16"), "mdc": ("sbuf", [128, 16], "bfloat16"),
    "pcol": ("sbuf", [128, 1], "int32"), "p15": ("sbuf", [128, 1], "int32"), "p15f": ("sbuf", [128, 1], "float32"),
    "fac": ("sbuf", [128, 1], "float32"), "fsq": ("sbuf", [128, 1], "float32"), "nsq": ("sbuf", [128, 1], "float32"),
    "q24": ("sbuf", [128, L], "float32"), "uli": ("sbuf", [128, 8], "int32"), "ul": ("sbuf", [128, 8], "uint16"),
    "scab": ("sbuf", [128, 2 * C], "bfloat16"), "ab": ("sbuf", [128, 2 * C], "bfloat16"),
    "lou": ("sbuf", [128, 2 * L], "uint16"), "hiu": ("sbuf", [128, 2 * L], "uint16"),
    "sw": ("sbuf", [128, C], "float32"), "gg": ("sbuf", [128, 2 * C], "float32"),
    "tb": ("sbuf", [128, 4 * C], "bfloat16"), "tp": ("sbuf", [128, 4 * C], "bfloat16"), "tob": ("sbuf", [128, 4 * C], "bfloat16"),
    "gb": ("sbuf", [128, 4 * C], "bfloat16"), "zt": ("sbuf", [128, 4 * C], "bfloat16"),
    "qz": ("sbuf", [128, C], "float8_e4m3fn_x4"), "sz": ("sbuf", [128, C], "uint8"),
    "rs": ("sbuf", [128, 4 * C], "float32"), "cof": ("sbuf", [128, C], "float32"), "yb": ("sbuf", [128, C], "float32"),
}
for _k in ("qu0", "qu", "qv"):
    SCRATCH[_k] = ("sbuf", [128, 128], "float8_e4m3fn_x4")
for _k in ("su0", "su", "sv"):
    SCRATCH[_k] = ("sbuf", [128, 128], "uint8")
for _k in ("cin", "minp", "pin"):
    SCRATCH[_k] = ("sbuf", [128, L], "int32")
for _k in ("cu", "mu", "au", "ciu", "acu", "fu", "alu", "beu", "wu", "ou"):
    SCRATCH[_k] = ("sbuf", [128, L], "uint16")
for _k in ("iob", "cb", "mb", "bb", "bmb", "fb", "hb", "n0b", "shb", "alb", "gab", "wb", "kb", "ob", "sc0", "sc1", "sc2"):
    SCRATCH[_k] = ("sbuf", [128, C], "bfloat16")
for _k in ("base", "alt", "mn", "mx", "lt", "dd", "yy", "yd", "sf", "dp", "p0", "sq", "pr", "rr"):
    SCRATCH[_k] = ("sbuf", [128, 2 * L], "float32")
for _d in range(ROUNDS + 1):
    SCRATCH["xt%d" % _d] = ("sbuf", [128, 4 * C], "bfloat16")
    SCRATCH["qx%d" % _d] = ("sbuf", [128, C], "float8_e4m3fn_x4")
    SCRATCH["sx%d" % _d] = ("sbuf", [128, C], "uint8")
for _d in range(ROUNDS):
    SCRATCH["lc%d" % _d] = ("sbuf", [128, C], "float8_e4m3fn_x4")
    SCRATCH["ls%d" % _d] = ("sbuf", [128, C], "uint8")
    SCRATCH["la%d" % _d] = ("sbuf", [128, L], "uint16")
    SCRATCH["lk%d" % _d] = ("sbuf", [128, L], "uint16")
    SCRATCH["off%d" % _d] = ("sbuf", [128, 2 * L], "uint16")
    SCRATCH["ku%d" % _d] = ("sbuf", [128, L], "uint16")
for _b in range(8):
    SCRATCH["ps%d" % _b] = ("psum", [128, 512], "float32")

SEMAPHORES = ["ev", "es", "et", "ep", "sent"] + ["d%d" % _k for _k in range(18)]
SEMAPHORES += ["%s%d" % (_k, _d) for _d in range(ROUNDS) for _k in ("ac", "aa", "ak")]

ADD, SUB, MUL, MIN, MAX = AluOpType.add, AluOpType.subtract, AluOpType.mult, AluOpType.min, AluOpType.max
GE, LT, EQ, NE = AluOpType.is_ge, AluOpType.is_lt, AluOpType.is_equal, AluOpType.not_equal
AND = AluOpType.bitwise_and
COPY = ActivationFunctionType.Copy


def rank_program(g, core, T, topo):
    rank = T.rank_of(core)
    if rank is None:
        return
    n = len(T.cores)
    queue = {"v": g.vector, "s": g.scalar, "t": g.tensor, "p": g, "y": g.sync}
    total, seen, wrote, read = {}, {}, {}, {}
    ndma = [0]

    def wait(q, toks):
        need = {}
        for s, k in toks:
            need[s] = max(need.get(s, 0), k)
        for s in need:
            if seen.get((q, s), 0) < need[s]:
                queue[q].wait_ge(T.sem[s], need[s])
                seen[(q, s)] = need[s]

    def before(q, rd, wr):
        toks = [wrote[r] for r in rd if r in wrote]
        for w in wr:
            toks += [wrote[w]] if w in wrote else []
            toks += read.get(w, [])
        wait(q, toks)

    def after(tok, rd, wr):
        for r in rd:
            read.setdefault(r, []).append(tok)
        for w in wr:
            wrote[w] = tok
            read[w] = []

    def op(q, rd, wr, f):
        before(q, rd, wr)
        s = "e" + q
        f(queue[q]).then_inc(T.sem[s], 1)
        total[s] = total.get(s, 0) + 1
        after((s, total[s]), rd, wr)

    def dma(q, rd, wr, out, in_):
        before(q, rd, wr)
        s = "d%d" % ndma[0]
        ndma[0] += 1
        queue[q].dma_start(out, in_).then_inc(T.sem[s], 16)
        after((s, 16), rd, wr)
        return q, (s, 16)

    def send(dst, rd, out, in_, rsem):
        before("p", rd, [])
        rid, pid = topo.addr(dst)[:2]
        g.remote_dma(out, in_, T.sem[rsem], T.sem.sent, pid, rid, topo.mask(core, dst))
        total["sent"] = total.get("sent", 0) + len(topo.engines(core, dst))

    def tt(out, a, b, o, rd, wr):
        op("v", rd, wr, lambda e: e.tensor_tensor(out, a, b, o))

    def ts(out, a, s1, o1, rd, wr, s2=None, o2=None):
        if o2 is None:
            op("v", rd, wr, lambda e: e.tensor_scalar(out, a, s1, None, o1))
        else:
            op("v", rd, wr, lambda e: e.tensor_scalar(out, a, s1, s2, o1, o2))

    def cp(q, out, a, rd, wr, scale=None):
        if q == "v":
            op("v", rd, wr, lambda e: e.tensor_copy(out, a))
        elif scale is None:
            op("s", rd, wr, lambda e: e.activation(out, a, COPY))
        else:
            op("s", rd, wr, lambda e: e.activation(out, a, COPY, scale=scale))

    def gather(q, out, win, lst):
        cp(q, T[out][:, :], T[win][:, :].indirect(T[lst][:, 0:L]), [win, lst], [out])

    def scatter(out, lst, src):
        op("v", [src, lst], [out], lambda e: e.tensor_copy(T[out][:, :].indirect(T[lst][:, 0:L]), T[src][:, :]))

    def scan(src, tmp):
        op("v", [src, "md"], [tmp], lambda e: e.tensor_tensor_scan(T[tmp][:, :], T.md[:, 0:2 * C:2], T[src][:, :], 0.0, MUL, ADD))

    def wrapped(out, tmp, wr):
        ts(out, T[tmp][:, 15:C:16], T.fac[:, :], MUL, [tmp, "fac"], wr, 192.0, ADD)

    def quant(qn, sn, xn, h, a, b, rd):
        op("v", rd, ["%s:%d" % (qn, h)], lambda e: e.quantize_mx(T[qn][:, a:b], T[sn][:, a:b], T[xn][:, 4 * a:4 * b]))

    def mm(bank, w, ws, x, xs, lo, hi, rd):
        op("t", rd, ["ps%d" % bank], lambda e: e.matmul_mx(T["ps%d" % bank][:, 0:hi - lo], w, ws, T[x][:, lo:hi], T[xs][:, lo:hi], True, True))

    def block(q, b):
        return T[q][:, 128 * b:128 * b + 128]

    dma("y", [], ["xt0a"], T.xt0[:, 0:4 * FIRST], T.x[:, 0:4 * FIRST])
    dma("s", [], ["cin"], T.cin[:, :], T.cl[:, :])
    dma("y", [], ["minp"], T.minp[:, :], T.ml[:, :])
    dma("s", [], ["pin"], T.pin[:, :], T.pl[:, :])
    dma("y", [], ["xt0b"], T.xt0[:, 4 * FIRST:4 * C], T.x[:, 4 * FIRST:4 * C])
    dma("y", [], ["uin"], T.uin[:, :], T.u[:, :])
    wait("y", [wrote["xt0b"]])
    dma("y", [], ["wcb"], T.wcb[:, :].bitcast(dt.uint8), T.wc[:, :])
    dma("y", [], ["wsb"], T.wsb[:, :], T.ws[:, :])
    dma("y", [], ["vin"], T.vin[:, :], T.v[:, :])

    op("p", [], ["r16"], lambda e: e.iota(T.r16[:, :], [[1, 16]], 128, -1))
    op("p", [], ["pcol"], lambda e: e.iota(T.pcol[:, :], [[0, 1]], 0, 1))
    op("v", [], ["ones"], lambda e: e.memset(T.ones[:, :], 1.0))
    op("p", ["ones"], ["eb0"], lambda e: e.affine_select(T.eb[:, 0:512], T.ones[:, :], [[-1, 128], [1000, 4]], EQ, 0.0, 0, 1))
    op("p", [], ["iob"], lambda e: e.iota(T.iob[:, :], [[1, C]], -192, 0, allow_small_or_imprecise_dtypes=True))
    op("p", [], ["q24"], lambda e: e.iota(T.q24[:, :], [[16, L]], 0, 0, allow_small_or_imprecise_dtypes=True))
    op("p", [], ["uli"], lambda e: e.iota(T.uli[:, :], [[16, 8]], 0, 0))
    for b in range(1, 4):
        a = 512 * b
        cp("s", T.eb[:, a + b:a + 512], T.eb[:, 0:512 - b], ["eb0"], ["eb%d" % b])
        cp("s", T.eb[:, a:a + b], T.eb[:, 512 - b:512], ["eb0"], ["eb%d:0" % b])
    ts(T.r15[:, :], T.r16[:, :], 15, AND, ["r16"], ["r15"])
    ts(T.p15[:, :], T.pcol[:, :], 15, AND, ["pcol"], ["p15"])
    ts(T.mda[:, :], T.r15[:, :], 1.0, EQ, ["r15"], ["mda"], BIG, MUL)
    ts(T.mdb[:, :], T.r15[:, :], 0.0, NE, ["r15"], ["mdb"])
    ts(T.fac[:, :], T.p15[:, :], 15.0, EQ, ["p15"], ["fac"], 1.0 / BIG, MAX)
    tt(T.md[:, 0:32:2], T.mda[:, :], T.mdb[:, :], MAX, ["mda", "mdb"], ["md"])
    ts(T.mdc[:, :], T.mdb[:, :], 2.0, MUL, ["mdb"], ["mdc"])
    cp("v", T.p15f[:, :], T.p15[:, :], ["p15"], ["p15f"])
    tt(T.fsq[:, :], T.fac[:, :], T.fac[:, :], MUL, ["fac"], ["fsq"])
    ts(T.md[:, 1:32:2], T.mdc[:, :], -1.0, ADD, ["mdc"], ["md1"])
    ts(T.nsq[:, :], T.fsq[:, :], -2.0, MUL, ["fsq"], ["nsq"])
    k = 32
    while k < 2 * C:
        w = min(k, 2 * C - k)
        cp("v", T.md[:, k:k + w], T.md[:, 0:w], ["md", "md1"], ["md"])
        k += w
    ts(T.base[:, 0:L], T.q24[:, :], T.p15f[:, :], ADD, ["q24", "p15f"], ["base0"])
    cp("v", T.ul[:, :], T.uli[:, :], ["uli"], ["ul"])

    cp("v", T.cu[:, :], T.cin[:, :], ["cin"], ["cu"])
    quant("qx0", "sx0", "xt0", 0, 0, FIRST, ["xt0a"])
    send(T.cores[(rank + 1) % n], ["qx0:0"], T.lc0[:, 0:FIRST].bitcast(dt.uint8), T.qx0[:, 0:FIRST].bitcast(dt.uint8), "ac0")
    gather("s", "cb", "iob", "cu")
    cp("v", T.mu[:, :], T.minp[:, :], ["minp"], ["mu"])
    scatter("alb", "cu", "iob")
    gather("s", "gab", "cb", "mu")
    gather("s", "mb", "iob", "mu")
    cp("v", T.au[:, :], T.pin[:, :], ["pin"], ["au"])
    scan("alb", "sc0")
    wrapped(T.ciu[:, :], "sc0", ["ciu"])
    wrapped(T.base[:, L:2 * L], "sc0", ["base1"])
    quant("qx0", "sx0", "xt0", 1, FIRST, C, ["xt0b"])
    gather("s", "hb", "gab", "ciu")
    gather("s", "fb", "mb", "ciu")
    scatter("bb", "au", "cb")

    def tables(part):
        rd = ["base0", "base1", "alt0", "alt1"]
        if part == 0:
            tt(T.mx[:, :], T.base[:, :], T.alt[:, :], MAX, rd, ["mx"])
            tt(T.mn[:, :], T.base[:, :], T.alt[:, :], MIN, rd, ["mn"])
            cp("v", T.hiu[:, :], T.mx[:, :], ["mx"], ["hiu"])
            cp("v", T.lou[:, :], T.mn[:, :], ["mn"], ["lou"])
        elif part == 1:
            tt(T.lt[:, :], T.base[:, :], T.alt[:, :], LT, rd, ["lt"])
            tt(T.dd[:, :], T.alt[:, :], T.base[:, :], SUB, rd, ["dd"])
        elif part == 2:
            tt(T.yy[:, 0:L], T.lt[:, 0:L], T.lt[:, L:2 * L], NE, ["lt"], ["yy0"])
            tt(T.yy[:, L:2 * L], T.lt[:, 0:L], T.lt[:, L:2 * L], NE, ["lt"], ["yy1"])
        elif part == 3:
            ts(T.sf[:, :], T.yy[:, :], T.nsq[:, :], MUL, ["yy0", "yy1", "nsq", "fsq"], ["sf"], T.fsq[:, :], ADD)
            tt(T.yd[:, :], T.yy[:, :], T.dd[:, :], MUL, ["yy0", "yy1", "dd"], ["yd"])
        else:
            tt(T.dp[:, :], T.sf[:, :], T.dd[:, :], MUL, ["sf", "dd"], ["dp"])
            tt(T.p0[:, :], T.base[:, :], T.yd[:, :], ADD, ["base0", "base1", "yd"], ["p0"])

    def state(d):
        for h in range(2):
            quant("qx%d" % d, "sx%d" % d, "xt%d" % d, h, HALF * h, HALF * h + HALF, ["xt%d:%d" % (d, b) for b in range(4)])

    stores = []
    for d in range(ROUNDS):
        last = d == ROUNDS - 1
        to = T.cores[(rank + d + 1) % n]
        q, sx, lc, ls, x1 = "qx%d" % d, "sx%d" % d, "lc%d" % d, "ls%d" % d, "xt%d" % (d + 1)
        la, lk, off, ku = "la%d" % d, "lk%d" % d, "off%d" % d, "ku%d" % d
        qq = [q + ":0", q + ":1"]
        lo = 0 if d else FIRST
        if d:
            state(d)
        send(to, qq, T[lc][:, lo:C].bitcast(dt.uint8), T[q][:, lo:C].bitcast(dt.uint8), "ac%d" % d)
        send(to, qq, T[ls][:, :], T[sx][:, :], "ac%d" % d)
        nl = len(topo.engines(core, to))
        wrote[lc], wrote[la], wrote[lk] = ("ac%d" % d, (2 if d else 3) * nl), ("aa%d" % d, nl), ("ak%d" % d, nl)
        if d == 0:
            op("v", ["uin"], ["qu0"], lambda e: e.quantize_mx(T.qu0[:, :], T.su0[:, :], T.uin[:, :]))
            op("v", ["qu0", "ul"], ["qu"], lambda e: e.tensor_copy(T.qu[:, :].bitcast(dt.uint32), T.qu0[:, :].bitcast(dt.uint32).indirect(T.ul[:, :])))
            cp("s", T.su[:, :], T.su0[:, :].indirect(T.ul[:, :]), ["qu0", "ul"], ["su"])
            gather("s", "ob", "iob", "au")
            gather("s", "wb", "ob", "ciu")
        for h in range(2):
            mm(h, T.qu[:, :], T.su[:, :], q, sx, HALF * h, HALF * h + HALF, ["qu", "su"] + (qq[h:h + 1] if d else qq))
        if d == 0:
            scan("hb", "sc1")
            scan("fb", "sc2")
            wrapped(T.alt[:, 0:L], "sc1", ["alt0"])
            wrapped(T.alt[:, L:2 * L], "sc2", ["alt1"])
            tables(0)
        cp("v", T.sw[:, 0:HALF], T.ps0[:, 0:HALF], ["ps0"], ["sw0"])
        cp("s", T.sw[:, HALF:C], T.ps1[:, 0:HALF], ["ps1"], ["sw1"])
        tables(1)
        sw, s2 = T.sw[:, :], ["sw0", "sw1"]
        if d == 0:
            cp("s", T.gg[:, 0:C], sw.indirect(T.hiu[:, 0:L]), s2 + ["hiu"], ["gg0", "gg1"])
            op("v", ["eb0"] + ["eb%d%s" % (b, e) for b in (1, 2, 3) for e in ("", ":0")], ["qe"], lambda e: e.quantize_mx(T.qe[:, :], T.se[:, :], T.eb[:, :]))
        else:
            cp("s", T.gg[:, 0:HALF], sw.indirect(T.hiu[:, 0:L // 2]), s2 + ["hiu"], ["gg0"])
            cp("v", T.gg[:, HALF:C], sw.indirect(T.hiu[:, L // 2:L]), s2 + ["hiu"], ["gg1"])
        cp("s", T.gg[:, C:2 * C], sw.indirect(T.hiu[:, L:2 * L]), s2 + ["hiu"], ["gg2"])
        for b in range(4):
            mm(2 + b, block("qe", b), block("se", b), q, sx, 0, C, ["qe"] + qq)
        tables(2)
        tt(T.ab[:, 0:2 * C:2], sw.indirect(T.lou[:, 0:L]), T.gg[:, 0:C], GE, s2 + ["lou", "gg0", "gg1"], ["ab0"])
        if d == 0:
            scan("wb", "sc0")
            gather("s", "bmb", "bb", "mu")
        tt(T.ab[:, 1:2 * C:2], sw.indirect(T.lou[:, L:2 * L]), T.gg[:, C:2 * C], GE, s2 + ["lou", "gg2"], ["ab1"])
        if d == 0:
            wrapped(T.acu[:, :], "sc0", ["acu"])
            gather("s", "n0b", "bmb", "acu")
        else:
            gather("s", "n0b", "gab", "beu")
        tables(3)
        op("v", ["ab0", "ab1", "md"], ["scab"], lambda e: e.tensor_tensor_scan(T.scab[:, :], T.md[:, :], T.ab[:, :], 0.0, MUL, ADD))
        tables(4)
        w = T.scab[:, 31:2 * C:32]
        tt(T.sq[:, 0:L], w, w, MUL, ["scab"], ["sq0"])
        tt(T.sq[:, L:2 * L], w, w, MUL, ["scab"], ["sq1"])
        tt(T.pr[:, :], T.sq[:, :], T.dp[:, :], MUL, ["sq0", "sq1", "dp"], ["pr"])
        tt(T.rr[:, :], T.p0[:, :], T.pr[:, :], ADD, ["p0", "pr"], ["rr"])
        cp("v", T[off][:, :], T.rr[:, :], ["rr"], [off])
        send(to, [off], T[la][:, :], T[off][:, L:2 * L], "aa%d" % d)
        for b in range(4):
            cp("s", T.tb[:, C * b:C * b + C], T["ps%d" % (2 + b)][:, 0:C], ["ps%d" % (2 + b)], ["tb%d" % b])
        gather("s", "shb", "iob", off)
        gather("v", "wb", "n0b", off)
        scan("wb", "sc0")
        wrapped(T.wu[:, :], "sc0", ["wu"])
        gather("s", "ob", "shb", "cu")
        gather("v", "kb", "shb", "wu")
        scan("kb", "sc1")
        wrapped(T[ku][:, :], "sc1", [ku])
        send(to, [ku], T[lk][:, :], T[ku][:, :], "ak%d" % d)
        bank = [6, 7, 0, 1]
        for b in range(4):
            mm(bank[b], block("qe", b), block("se", b), lc, ls, 0, C, ["qe", lc])
        scan("ob", "sc2")
        if not last:
            gather("s", "alb", "shb", "ciu")
            gather("s", "fb", "kb", "ciu")
            scan("fb", "sc0")
            wrapped(T.ou[:, :], "sc2", ["ou"])
            wrapped(T.fu[:, :], "sc0", ["fu"])
            wrapped(T.alt[:, L:2 * L], "sc0", ["alt1"])
            gather("v", "hb", "cb", "fu")
            scan("alb", "sc1")
            scan("hb", "sc2")
            wrapped(T.alu[:, :], "sc1", ["alu"])
            wrapped(T.alt[:, 0:L], "sc2", ["alt0"])
            tables(0)
        else:
            wrapped(T.ou[:, :], "sc2", ["ou"])
            ts(T.cof[:, :], T.kb[:, :], 192.0, ADD, ["kb"], ["cof"])
            stores.append(dma("y", ["cof"], [], T.co[:, :], T.cof[0:128:16, :]))
            op("v", ["vin"], ["qv"], lambda e: e.quantize_mx(T.qv[:, :], T.sv[:, :], T.vin[:, :]))

        def arrived(b):
            cp("s", T.tp[:, C * b:C * b + C], T["ps%d" % bank[b]][:, 0:C], ["ps%d" % bank[b]], ["tp%d" % b], 0.5)
        arrived(0)
        for b in range(4):
            s = slice(C * b, C * b + C)
            if b < 3:
                arrived(b + 1)
            cp("s", T.gb[:, s], T.tp[:, s].indirect(T[la][:, :]), ["tp%d" % b, la], ["gb%d" % b])
            tt(T.zt[:, b:4 * C:4], T.tp[:, s].indirect(T[lk][:, :]), T.gb[:, s], ADD, ["tp%d" % b, lk, "gb%d" % b], ["zt%d" % b])
        for b in (2, 3):
            s = slice(C * b, C * b + C)
            cp("s", T.tob[:, s], T.tb[:, s].indirect(T.ou[:, :]), ["tb%d" % b, "ou"], ["tob%d" % b], 32.0)
        for h in range(2):
            quant("qz", "sz", "zt", h, HALF * h, HALF * h + HALF, ["zt%d" % b for b in range(4)])
        if not last:
            gather("s", "alb", "hb", "alu")
        at = {}
        for i, b in enumerate((2, 0, 3, 1)):
            for h in range(2):
                at[(b, h)] = k = (2 * i + h + 6) % 8
                mm(k, block("wcb", b), block("wsb", b), "qz", "sz", HALF * h, HALF * h + HALF, ["wcb", "wsb", "qz:%d" % h])

        def bring(b):
            for h in range(2):
                a, ps = C * b + HALF * h, "ps%d" % at[(b, h)]
                if b < 2:
                    cp("s", T.rs[:, a:a + HALF], T[ps][:, 0:HALF], [ps], ["rs%d:%d" % (b, h)], 0.03125)
                else:
                    tt(T.rs[:, a:a + HALF], T[ps][:, 0:HALF], T.tob[:, a:a + HALF], ADD, [ps, "tob%d" % b], ["rs%d:%d" % (b, h)])

        def finish(b):
            s = slice(C * b, C * b + C)
            rd, wr = ["rs%d:0" % b, "rs%d:1" % b, off], ["%s:%d" % (x1, b)]
            picked = T.rs[:, s].indirect(T[off][:, L:2 * L])
            if b < 2:
                tt(T[x1][:, b:4 * C:4], picked, T.tb[:, s], ADD, rd + ["tb%d" % b], wr)
            else:
                cp("s", T[x1][:, b:4 * C:4], picked, rd, wr, 0.03125)
        bring(2)
        bring(0)
        if not last:
            scan("alb", "sc1")
            wrapped(T.beu[:, :], "sc1", ["beu"])
        finish(0)
        finish(2)
        bring(1)
        bring(3)
        finish(1)
        finish(3)
        if not last:
            gather("s", "gab", "cb", off)

    d = ROUNDS
    state(d)
    q, sx = "qx%d" % d, "sx%d" % d
    qq = [q + ":0", q + ":1"]

    def scales(queue_name, i):
        stores.append(dma(queue_name, qq, [], T.osc[4 * i:4 * i + 4, :], T[sx][32 * i:32 * i + 4, :]))
    for h in range(2):
        mm(h, T.qv[:, :], T.sv[:, :], q, sx, HALF * h, HALF * h + HALF, ["qv", qq[h]])
    stores.append(dma("y", qq, [], T.oc[:, :], T[q][:, :].bitcast(dt.uint8)))
    scales("y", 0)
    scales("y", 1)
    cp("v", T.yb[:, 0:HALF], T.ps0[:, 0:HALF], ["ps0"], ["yb0"])
    cp("s", T.yb[:, HALF:C], T.ps1[:, 0:HALF], ["ps1"], ["yb1"])
    stores.append(dma("y", ["yb0"], [], T.y[:, 0:HALF], T.yb[:, 0:HALF]))
    stores.append(dma("s", ["yb1"], [], T.y[:, HALF:C], T.yb[:, HALF:C]))
    scales("s", 2)
    scales("s", 3)
    for q, tok in stores:
        wait(q, [tok])
    wait("p", [(s, total[s]) for s in ("ev", "es", "et", "ep", "sent")])
